import numpy as np, ml_dtypes
CORES = [2,130,258,386,10,138,266,394,18,146,274,402,26,154,282,410,34,162,290,418,42,170,298,426,50,178,306,434,58,186,314,442]
N = 32
GROUPS = [[0,1,2,3],[4,5,6,7],[8,9,10,11],[12,13,14,15],[16,17,18,19],[20,21,22,23],[24,25,26,27],[28,29,30,31]]
def setup_inputs(rng):
    return {"x": rng.standard_normal((N, 128, 64), dtype=np.float32).astype(ml_dtypes.bfloat16)}
def reference(x):
    y = np.empty((N, 128, 256), x.dtype)
    for g in GROUPS:
        s = np.concatenate([x[r] for r in g], axis=1)
        for r in g:
            y[r] = s
    return {"y": y}

@@ -1,0 +1,55 @@
+from concourse.bass import DstId, RemoteDMATransfer
+
+SCRATCH = {
+    "gat": ("dram", [4, 128, 64], "bfloat16"),
+}
+SEMAPHORES = ["loaded", "stored", "sent", "a_prev", "a_next", "a_diag"]
+
+
+def rank_program(g, core, T, topo):
+    rank = T.rank_of(core)
+    if rank is None:
+        return
+    group = [m for m in T.tables["GROUPS"] if rank in m][0]
+    cores = [T.cores[r] for r in group]
+    by_host = {topo.host(c): j for j, c in enumerate(cores)}
+    h = topo.host(core)
+    p, prv, nxt, dia = (by_host[(h + d) % 4] for d in (0, 3, 1, 2))
+    w = T.x.shape[1]
+    sem = T.sem
+
+    def ycols(j):
+        return T.y[:, j * w:(j + 1) * w]
+
+    def dst(j):
+        rid, pid = topo.addr(cores[j], core)
+        return DstId(rid=rid, pnc=pid)
+
+    eng = topo.mask(core, cores[nxt])
+    n_eng = 8
+
+    g.dma_start(T.gat[p], T.x[:]).then_inc(sem.loaded, 16)
+    g.wait_ge(sem.loaded, 16)
+
+    g.remote_dma_fused([
+        RemoteDMATransfer(dst_ids=[dst(nxt)], dma_engine_mask=0x0F, remote_sem=sem.a_prev,
+                          src=T.gat[p], dst=T.gat[p]),
+        RemoteDMATransfer(dst_ids=[dst(prv)], dma_engine_mask=0xF0, remote_sem=sem.a_next,
+                          src=T.gat[p], dst=T.gat[p]),
+    ], local_sem=sem.sent)
+
+    g.dma_start(ycols(p), T.x[:]).then_inc(sem.stored, 16)
+
+    g.wait_ge(sem.a_prev, 4)
+    rid, pid = topo.addr(cores[nxt], core)
+    g.remote_dma(T.gat[prv], T.gat[prv], sem.a_diag, sem.sent, pid, rid, eng)
+
+    g.dma_start(ycols(prv), T.gat[prv]).then_inc(sem.stored, 16)
+    g.wait_ge(sem.a_next, 4)
+    g.dma_start(ycols(nxt), T.gat[nxt]).then_inc(sem.stored, 16)
+
+    g.wait_ge(sem.a_diag, n_eng)
+    g.dma_start(ycols(dia), T.gat[dia]).then_inc(sem.stored, 16)
+
+    g.wait_ge(sem.sent, 8 + n_eng)
+    g.wait_ge(sem.stored, 64)

@@ -3,7 +3,7 @@ from concourse.bass import DstId, RemoteDMATransfer
 SCRATCH = {
     "gat": ("dram", [4, 128, 64], "bfloat16"),
 }
-SEMAPHORES = ["loaded", "stored", "sent", "a_prev", "a_next", "a_diag"]
+SEMAPHORES = ["loaded", "stored", "sent", "a_rack", "a_cable", "a_diag"]
 
 
 def rank_program(g, core, T, topo):
@@ -12,9 +12,11 @@ def rank_program(g, core, T, topo):
         return
     group = [m for m in T.tables["GROUPS"] if rank in m][0]
     cores = [T.cores[r] for r in group]
-    by_host = {topo.host(c): j for j, c in enumerate(cores)}
-    h = topo.host(core)
-    p, prv, nxt, dia = (by_host[(h + d) % 4] for d in (0, 3, 1, 2))
+    p = group.index(rank)
+    others = [j for j in range(len(group)) if j != p]
+    dia = [j for j in others if not topo.may_write(core, cores[j])][0]
+    rck = [j for j in others if topo.same_plane(core, cores[j])][0]
+    cab = [j for j in others if j not in (dia, rck)][0]
     w = T.x.shape[1]
     sem = T.sem
 
@@ -25,31 +27,28 @@ def rank_program(g, core, T, topo):
         rid, pid = topo.addr(cores[j], core)
         return DstId(rid=rid, pnc=pid)
 
-    eng = topo.mask(core, cores[nxt])
-    n_eng = 8
-
     g.dma_start(T.gat[p], T.x[:]).then_inc(sem.loaded, 16)
     g.wait_ge(sem.loaded, 16)
 
     g.remote_dma_fused([
-        RemoteDMATransfer(dst_ids=[dst(nxt)], dma_engine_mask=0x0F, remote_sem=sem.a_prev,
+        RemoteDMATransfer(dst_ids=[dst(cab)], dma_engine_mask=0x0F, remote_sem=sem.a_cable,
                           src=T.gat[p], dst=T.gat[p]),
-        RemoteDMATransfer(dst_ids=[dst(prv)], dma_engine_mask=0xF0, remote_sem=sem.a_next,
+        RemoteDMATransfer(dst_ids=[dst(rck)], dma_engine_mask=0xF0, remote_sem=sem.a_rack,
                           src=T.gat[p], dst=T.gat[p]),
     ], local_sem=sem.sent)
 
     g.dma_start(ycols(p), T.x[:]).then_inc(sem.stored, 16)
 
-    g.wait_ge(sem.a_prev, 4)
-    rid, pid = topo.addr(cores[nxt], core)
-    g.remote_dma(T.gat[prv], T.gat[prv], sem.a_diag, sem.sent, pid, rid, eng)
+    g.wait_ge(sem.a_cable, 4)
+    rid, pid = topo.addr(cores[rck], core)
+    g.remote_dma(T.gat[cab], T.gat[cab], sem.a_diag, sem.sent, pid, rid, topo.mask(core, cores[rck]))
 
-    g.dma_start(ycols(prv), T.gat[prv]).then_inc(sem.stored, 16)
-    g.wait_ge(sem.a_next, 4)
-    g.dma_start(ycols(nxt), T.gat[nxt]).then_inc(sem.stored, 16)
+    g.dma_start(ycols(cab), T.gat[cab]).then_inc(sem.stored, 16)
+    g.wait_ge(sem.a_rack, 4)
+    g.dma_start(ycols(rck), T.gat[rck]).then_inc(sem.stored, 16)
 
-    g.wait_ge(sem.a_diag, n_eng)
+    g.wait_ge(sem.a_diag, 8)
     g.dma_start(ycols(dia), T.gat[dia]).then_inc(sem.stored, 16)
 
-    g.wait_ge(sem.sent, 8 + n_eng)
+    g.wait_ge(sem.sent, 16)
     g.wait_ge(sem.stored, 64)

from concourse.bass import DstId, RemoteDMATransfer

SCRATCH = {
    "gat": ("dram", [4, 128, 64], "bfloat16"),
}
SEMAPHORES = ["loaded", "stored", "sent", "a_rack", "a_cable", "a_diag"]


def rank_program(g, core, T, topo):
    rank = T.rank_of(core)
    if rank is None:
        return
    group = [m for m in T.tables["GROUPS"] if rank in m][0]
    cores = [T.cores[r] for r in group]
    p = group.index(rank)
    others = [j for j in range(len(group)) if j != p]
    dia = [j for j in others if not topo.may_write(core, cores[j])][0]
    rck = [j for j in others if topo.same_plane(core, cores[j])][0]
    cab = [j for j in others if j not in (dia, rck)][0]
    w = T.x.shape[1]
    sem = T.sem

    def ycols(j):
        return T.y[:, j * w:(j + 1) * w]

    def dst(j):
        rid, pid = topo.addr(cores[j], core)
        return DstId(rid=rid, pnc=pid)

    g.dma_start(T.gat[p], T.x[:]).then_inc(sem.loaded, 16)
    g.wait_ge(sem.loaded, 16)

    g.remote_dma_fused([
        RemoteDMATransfer(dst_ids=[dst(cab)], dma_engine_mask=0x0F, remote_sem=sem.a_cable,
                          src=T.gat[p], dst=T.gat[p]),
        RemoteDMATransfer(dst_ids=[dst(rck)], dma_engine_mask=0xF0, remote_sem=sem.a_rack,
                          src=T.gat[p], dst=T.gat[p]),
    ], local_sem=sem.sent)

    g.dma_start(ycols(p), T.x[:]).then_inc(sem.stored, 16)

    g.wait_ge(sem.a_cable, 4)
    rid, pid = topo.addr(cores[rck], core)
    g.remote_dma(T.gat[cab], T.gat[cab], sem.a_diag, sem.sent, pid, rid, topo.mask(core, cores[rck]))

    g.dma_start(ycols(cab), T.gat[cab]).then_inc(sem.stored, 16)
    g.wait_ge(sem.a_rack, 4)
    g.dma_start(ycols(rck), T.gat[rck]).then_inc(sem.stored, 16)

    g.wait_ge(sem.a_diag, 8)
    g.dma_start(ycols(dia), T.gat[dia]).then_inc(sem.stored, 16)

    g.wait_ge(sem.sent, 16)
    g.wait_ge(sem.stored, 64)
